import numpy as np
import ml_dtypes


def mxq(x, axis, fmt="e4m3"):
    dtype, down = {"e4m3": (ml_dtypes.float8_e4m3fn, 7), "e5m2": (ml_dtypes.float8_e5m2, 14)}[fmt]
    v = np.moveaxis(np.asarray(x, np.float32).astype(ml_dtypes.bfloat16).astype(np.float64), axis, -1)
    blocks = v.reshape(v.shape[:-1] + (-1, 32))
    amax = np.abs(blocks).max(-1, keepdims=True)
    byte = np.maximum(np.where(amax > 0, np.frexp(amax)[1] - 1 + 127, 0) - down, 1)
    scale = np.exp2(byte - 127.0)
    codes = (blocks / scale).astype(np.float32).astype(dtype).astype(np.float64)
    return np.moveaxis((codes * scale).reshape(v.shape), -1, axis)


WIDE = False


def mx_kscale(k):
    if not WIDE:
        return np.ones(k)
    levels = np.array([10, -10, 5, -5, 0])
    if k % 512:
        return np.exp2(np.random.permutation(np.resize(levels, k // 32))).repeat(32)
    a = np.empty((k // 512, 16))
    for p in range(k // 512):
        a[p, :8] = np.random.permutation(np.resize(levels, 8))
        for g in range(8):
            far = levels[np.abs(levels - a[p, g]) >= 10]
            a[p, g + 8] = far[np.random.randint(len(far))]
    return np.exp2(a.ravel()).repeat(32)


def f64(x):
    return np.asarray(x).astype(np.float64)


def striped(idx):
    return np.tile(idx.reshape(-1, 16).T, (8, 1)).astype(np.uint16)


def unstriped(offs):
    return offs[:16].T.reshape(-1).astype(np.int64)


E2M1 = np.array([0.0, 0.5, 1.0, 1.5, 2.0, 3.0, 4.0, 6.0, -0.0, -0.5, -1.0, -1.5, -2.0, -3.0, -4.0, -6.0])


def pack_fp4(w):
    k, n = w.shape
    w = f64(np.asarray(w, np.float32).astype(ml_dtypes.bfloat16)).reshape(k // 32, 32, n)
    amax = np.abs(w).max(1)
    mant, ex = np.frexp(amax / 6.0)
    byte = np.clip(np.where(amax > 0, np.where(mant > 0.5, ex, ex - 1) + 127, 1), 1, 254)
    scaled = (w * np.exp2(127.0 - byte)[:, None, :]).reshape(k, n).astype(np.float32)
    c = np.ascontiguousarray(scaled.reshape(k // 512, 128, 4, n).transpose(0, 1, 3, 2)).astype(ml_dtypes.float4_e2m1fn).view(np.uint8) & 0xF
    words = (c[..., 0::2] | (c[..., 1::2] << 4)).reshape(k // 512, 128, 2 * n)
    return np.ascontiguousarray(words), np.ascontiguousarray(byte.astype(np.uint8).reshape(k // 512, 16, n))


def unpack_fp4(words, scales):
    g, _, n = scales.shape
    words = np.ascontiguousarray(words).reshape(g, 128, n, 2)
    nib = np.empty((g, 128, n, 4), np.uint8)
    nib[..., 0::2] = words & 0xF
    nib[..., 1::2] = words >> 4
    vals = E2M1[nib] * np.repeat(np.exp2(scales.astype(np.float64) - 127.0), 8, axis=1)[..., None]
    return vals.transpose(0, 1, 3, 2).reshape(g * 512, n)


def relu(v):
    return np.maximum(v, 0.0)


def sigmoid(v):
    return 1.0 / (1.0 + np.exp(-np.maximum(v, -700.0)))

def planes(y):
    n, m = y.shape
    v = y.astype(np.float32).astype(ml_dtypes.bfloat16).astype(np.float64).reshape(n // 32, 32, m)
    top = np.abs(v).max(1)
    byte = np.clip(np.where(top > 0, np.frexp(top)[1] - 1 + 127 - 7, 1), 1, 254)
    codes = (v * np.exp2(127.0 - byte)[:, None, :]).reshape(n, m).astype(np.float32).astype(ml_dtypes.float8_e4m3fn).view(np.uint8)
    words = codes.reshape(n // 512, 128, 4, m).transpose(0, 1, 3, 2)
    return np.ascontiguousarray(words), np.ascontiguousarray(byte.astype(np.uint8).reshape(n // 512, 16, m))


K, T, N = 512, 512, 512


def setup_inputs():
    n = np.random.standard_normal
    s = mx_kscale(K)[:, None]
    packed_xT = pack_fp4(n((K, T)) * s)
    return {
        "x_words": packed_xT[0],
        "x_scales": packed_xT[1],
        "w1": (n((K, N)) / np.sqrt(K) / s).astype(np.float32),
        "w2": (n((K, N)) / np.sqrt(K) / s).astype(np.float32),
        "w3": (n((K, N)) / np.sqrt(K) / s).astype(np.float32),
        "pos1": striped(np.random.permutation(T)),
        "pos2": striped(np.random.permutation(T)),
    }


def reference(x_words, x_scales, w1, w2, w3, pos1, pos2):
    xq = unpack_fp4(x_words, x_scales)
    y = mxq(f64(w1), 0, "e4m3").T @ xq
    e = mxq(f64(w2), 0, "e4m3").T @ xq
    h = mxq(f64(w3), 0, "e4m3").T @ xq
    z = (sigmoid(y + e[:, unstriped(pos1)])) * h[:, unstriped(pos1)] + (sigmoid(y + e[:, unstriped(pos2)])) * h[:, unstriped(pos2)]
    out_0 = relu(z)
    return (out_0,) + planes(out_0)

@@ -1,0 +1,225 @@
+from contextlib import ExitStack
+
+import concourse.mybir as mybir
+
+K, T, N = 512, 512, 512
+FLOPS = 3 * 2 * K * T * N
+
+F32 = mybir.dt.float32
+BF16 = mybir.dt.bfloat16
+I32 = mybir.dt.int32
+U32 = mybir.dt.uint32
+U16 = mybir.dt.uint16
+U8 = mybir.dt.uint8
+FP8X4 = mybir.dt.float8_e4m3fn_x4
+FP4X4 = mybir.dt.float4_e2m1fn_x4
+ACT = mybir.ActivationFunctionType
+ALU = mybir.AluOpType
+
+P = 128
+PACK = 4
+SPARE = 8
+CHUNKS = ((0, 256), (256, 384), (384, 512))
+
+
+def tile_picked_wgatedg_relu_lo_kernel(
+    tc, x_words, x_scales, w1, w2, w3, pos1, pos2, out_0, out_1, out_2
+):
+    nc = tc.nc
+    with ExitStack() as ctx:
+        keep = ctx.enter_context(tc.tile_pool(name="keep", bufs=1))
+        psum = ctx.enter_context(tc.psum_pool(name="psum", bufs=8))
+
+        def sb(name, shape, dtype):
+            return keep.tile(shape, dtype, name=name, align_bytes=64)
+
+        lists = [sb("list%d" % d, [P, T // 16], U16) for d in range(2)]
+        xw = sb("xw", [P, 2 * T], U8)
+        xs = sb("xs", [P, T], U8)
+        zero = sb("zero", [P, SPARE], F32)
+        raw = {n: sb("raw_" + n, [P, PACK, N], F32) for n in "eyh"}
+        e_sb = [sb("e%d" % t, [P, T + SPARE], F32) for t in range(PACK)]
+        y_sb = [sb("y%d" % t, [P, T], F32) for t in range(PACK)]
+        h_sb = [sb("h%d" % t, [P, T], F32) for t in range(PACK)]
+
+        nc.gpsimd.memset(xs[:].bitcast(I32), 0)
+        nc.gpsimd.memset(zero[:], 0.0)
+        for t in range(PACK):
+            nc.scalar.activation(e_sb[t][:, T:], zero[:], ACT.Sigmoid)
+
+        def load_w(n, w):
+            nc.sync.dma_start(out=raw[n][:], in_=w.rearrange("(p j) c -> p j c", j=PACK))
+
+        load_w("e", w2)
+        nc.sync.dma_start(out=xw[:].bitcast(I32), in_=x_words[0].bitcast(I32))
+        for q in range(4):
+            nc.scalar.dma_start(
+                out=xs[32 * q : 32 * q + 4, :].bitcast(I32),
+                in_=x_scales[0, 4 * q : 4 * q + 4, :].bitcast(I32),
+            )
+        load_w("y", w1)
+        nc.sync.dma_start(lists[0][:], pos1)
+        nc.sync.dma_start(lists[1][:], pos2)
+        load_w("h", w3)
+
+        grouped = {}
+        stationary = {}
+
+        def cast(engine, n, t0, t1):
+            g = sb("g_%s%d" % (n, t0), [P, (t1 - t0) * N], BF16)
+            grouped[n, t0] = (g, t1)
+            src = raw[n][:].rearrange("p j (m t) -> p m t j", t=PACK)[:, :, t0:t1, :]
+            dst = g[:].rearrange("p (t m j) -> p m t j", m=P, j=PACK)
+            if engine == "vector":
+                nc.vector.tensor_copy(out=dst, in_=src)
+            else:
+                nc.scalar.copy(out=dst, in_=src)
+
+        def quantize(n, t0):
+            g, t1 = grouped[n, t0]
+            codes = sb("c_%s%d" % (n, t0), [P, (t1 - t0) * P], U32)
+            scales = sb("s_%s%d" % (n, t0), [P, (t1 - t0) * P], U8)
+            nc.vector.quantize_mx(out=codes[:].bitcast(FP8X4), scales=scales[:], in_=g[:])
+            for t in range(t0, t1):
+                cols = slice((t - t0) * P, (t - t0 + 1) * P)
+                stationary[n, t] = (codes[:, cols], scales[:, cols])
+
+        def project(n, t, dst):
+            codes, scales = stationary[n, t]
+            acc = psum.tile([P, T], F32, name="acc")
+            nc.tensor.matmul_mx(
+                out=acc[:],
+                lhsT=codes.bitcast(FP8X4),
+                lhsT_scale=scales,
+                rhs=xw[:].bitcast(FP4X4),
+                rhs_scale=xs[:],
+                start=True,
+                stop=True,
+            )
+            nc.scalar.copy(out=dst, in_=acc[:])
+
+        pre = {}
+        gate = {}
+
+        def gate_sum(t):
+            for d in range(2):
+                pre[t, d] = sb("pre%d_%d" % (t, d), [P, T], F32)
+                nc.vector.tensor_tensor(pre[t, d][:], e_sb[t][:].indirect(lists[d][:]), y_sb[t][:], ALU.add)
+
+        def gate_sigmoid(t):
+            for d in range(2):
+                gate[t, d] = sb("gate%d_%d" % (t, d), [P, T], F32)
+                nc.scalar.activation(gate[t, d][:], pre[t, d][:], ACT.Sigmoid)
+
+        msg = {
+            (c, d): sb("msg%d_%d" % (c, d), [P, PACK * (v1 - v0)], F32)
+            for c, (v0, v1) in enumerate(CHUNKS)
+            for d in range(2)
+        }
+
+        def messages(c, t):
+            v0, v1 = CHUNKS[c]
+            w = v1 - v0
+            for d in range(2):
+                nc.vector.tensor_tensor(
+                    msg[c, d][:, t * w : (t + 1) * w],
+                    h_sb[t][:].indirect(lists[d][:, v0 // 16 : v1 // 16]),
+                    gate[t, d][:, v0:v1],
+                    ALU.mult,
+                )
+
+        o_codes = sb("o_codes", [P, T], U32)
+        o_scales = sb("o_scales", [P, T], U8)
+        total = {}
+        rounded = {}
+        out_rows = out_0.rearrange("(p t) v -> p t v", t=PACK)
+        out_words = out_1[0].rearrange("p c r -> p (c r)").bitcast(I32)
+
+        def add_up(c):
+            v0, v1 = CHUNKS[c]
+            total[c] = sb("total%d" % c, [P, PACK * (v1 - v0)], F32)
+            nc.vector.tensor_tensor(total[c][:], msg[c, 0][:], msg[c, 1][:], ALU.add)
+
+        def round_out(c, engine):
+            v0, v1 = CHUNKS[c]
+            rounded[c] = sb("rounded%d" % c, [P, PACK * (v1 - v0)], BF16)
+            src = total[c][:].rearrange("p (t c i) -> p c t i", t=PACK, i=4)
+            dst = rounded[c][:].rearrange("p (c i t) -> p c t i", t=PACK, i=4)
+            if engine == "vector":
+                nc.vector.tensor_scalar_max(dst, src, 0.0)
+            else:
+                nc.scalar.activation(dst, src, ACT.Relu)
+
+        def store_result(c):
+            v0, v1 = CHUNKS[c]
+            res = sb("res%d" % c, [P, PACK * (v1 - v0)], F32)
+            nc.scalar.activation(res[:], total[c][:], ACT.Relu)
+            nc.sync.dma_start(out=out_rows[:, :, v0:v1], in_=res[:].rearrange("p (t v) -> p t v", t=PACK))
+
+        def store_codes(c):
+            v0, v1 = CHUNKS[c]
+            nc.vector.quantize_mx(
+                out=o_codes[:, v0:v1].bitcast(FP8X4), scales=o_scales[:, v0:v1], in_=rounded[c][:]
+            )
+            nc.sync.dma_start(out=out_words[:, v0:v1], in_=o_codes[:, v0:v1].bitcast(I32))
+
+        cast("vector", "e", 0, 2)
+        cast("scalar", "e", 2, 4)
+        quantize("e", 0)
+        project("e", 0, e_sb[0][:, :T])
+        quantize("e", 2)
+        cast("vector", "y", 0, 1)
+        cast("scalar", "y", 2, 4)
+        quantize("y", 0)
+        project("y", 0, y_sb[0][:])
+        cast("vector", "y", 1, 2)
+        quantize("y", 1)
+        quantize("y", 2)
+        project("e", 1, e_sb[1][:, :T])
+        project("y", 1, y_sb[1][:])
+        gate_sum(0)
+        cast("scalar", "h", 0, 2)
+        quantize("h", 0)
+        gate_sigmoid(0)
+        gate_sum(1)
+        project("h", 0, h_sb[0][:])
+        project("e", 2, e_sb[2][:, :T])
+        project("y", 2, y_sb[2][:])
+        gate_sigmoid(1)
+        project("h", 1, h_sb[1][:])
+        messages(0, 0)
+        gate_sum(2)
+        cast("scalar", "h", 2, 4)
+        quantize("h", 2)
+        project("e", 3, e_sb[3][:, :T])
+        project("y", 3, y_sb[3][:])
+        messages(0, 1)
+        gate_sigmoid(2)
+        gate_sum(3)
+        project("h", 2, h_sb[2][:])
+        project("h", 3, h_sb[3][:])
+        gate_sigmoid(3)
+        messages(0, 2)
+        messages(0, 3)
+        add_up(0)
+        round_out(0, "scalar")
+        store_result(0)
+        for t in range(PACK):
+            messages(1, t)
+        add_up(1)
+        store_codes(0)
+        round_out(1, "scalar")
+        store_result(1)
+        for t in range(PACK):
+            messages(2, t)
+        add_up(2)
+        store_codes(1)
+        round_out(2, "vector")
+        store_result(2)
+        store_codes(2)
+        for q in range(4):
+            queue = nc.scalar if q % 2 else nc.sync
+            queue.dma_start(
+                out=out_2[0, 4 * q : 4 * q + 4, :].bitcast(I32),
+                in_=o_scales[32 * q : 32 * q + 4, :].bitcast(I32),
+            )

@@ -1,6 +1,7 @@
 from contextlib import ExitStack
 
 import concourse.mybir as mybir
+from concourse.masks import make_identity
 
 K, T, N = 512, 512, 512
 FLOPS = 3 * 2 * K * T * N
@@ -19,7 +20,7 @@ ALU = mybir.AluOpType
 P = 128
 PACK = 4
 SPARE = 8
-CHUNKS = ((0, 256), (256, 384), (384, 512))
+CHUNKS = ((0, 384), (384, 512))
 
 
 def tile_picked_wgatedg_relu_lo_kernel(
@@ -28,10 +29,10 @@ def tile_picked_wgatedg_relu_lo_kernel(
     nc = tc.nc
     with ExitStack() as ctx:
         keep = ctx.enter_context(tc.tile_pool(name="keep", bufs=1))
-        psum = ctx.enter_context(tc.psum_pool(name="psum", bufs=8))
+        psum = ctx.enter_context(tc.psum_pool(name="psum", bufs=1))
 
-        def sb(name, shape, dtype):
-            return keep.tile(shape, dtype, name=name, align_bytes=64)
+        def sb(name, shape, dtype, tag=""):
+            return keep.tile(shape, dtype, name=name, tag=tag or name, align_bytes=64)
 
         lists = [sb("list%d" % d, [P, T // 16], U16) for d in range(2)]
         xw = sb("xw", [P, 2 * T], U8)
@@ -42,23 +43,26 @@ def tile_picked_wgatedg_relu_lo_kernel(
         y_sb = [sb("y%d" % t, [P, T], F32) for t in range(PACK)]
         h_sb = [sb("h%d" % t, [P, T], F32) for t in range(PACK)]
 
-        nc.gpsimd.memset(xs[:].bitcast(I32), 0)
-        nc.gpsimd.memset(zero[:], 0.0)
+        nc.vector.memset(xs[:].bitcast(I32), 0)
+        nc.vector.memset(zero[:], 0.0)
         for t in range(PACK):
             nc.scalar.activation(e_sb[t][:, T:], zero[:], ACT.Sigmoid)
+
+        ident = sb("ident", [P, P], F32)
+        make_identity(nc, ident[:])
 
         def load_w(n, w):
             nc.sync.dma_start(out=raw[n][:], in_=w.rearrange("(p j) c -> p j c", j=PACK))
 
-        load_w("e", w2)
         nc.sync.dma_start(out=xw[:].bitcast(I32), in_=x_words[0].bitcast(I32))
+        nc.sync.dma_start(lists[0][:], pos1)
+        load_w("e", w2)
         for q in range(4):
-            nc.scalar.dma_start(
+            nc.sync.dma_start(
                 out=xs[32 * q : 32 * q + 4, :].bitcast(I32),
                 in_=x_scales[0, 4 * q : 4 * q + 4, :].bitcast(I32),
             )
         load_w("y", w1)
-        nc.sync.dma_start(lists[0][:], pos1)
         nc.sync.dma_start(lists[1][:], pos2)
         load_w("h", w3)
 
@@ -84,19 +88,19 @@ def tile_picked_wgatedg_relu_lo_kernel(
                 cols = slice((t - t0) * P, (t - t0 + 1) * P)
                 stationary[n, t] = (codes[:, cols], scales[:, cols])
 
-        def project(n, t, dst):
+        def project(n, t, dst, bank, v0=0, v1=T):
             codes, scales = stationary[n, t]
-            acc = psum.tile([P, T], F32, name="acc")
+            acc = psum.tile([P, v1 - v0], F32, name="acc", tag="bank%d" % bank)
             nc.tensor.matmul_mx(
                 out=acc[:],
                 lhsT=codes.bitcast(FP8X4),
                 lhsT_scale=scales,
-                rhs=xw[:].bitcast(FP4X4),
-                rhs_scale=xs[:],
+                rhs=xw[:, 2 * v0 : 2 * v1].bitcast(FP4X4),
+                rhs_scale=xs[:, v0:v1],
                 start=True,
                 stop=True,
             )
-            nc.scalar.copy(out=dst, in_=acc[:])
+            nc.scalar.copy(out=dst[:, v0:v1], in_=acc[:])
 
         pre = {}
         gate = {}
@@ -104,23 +108,27 @@ def tile_picked_wgatedg_relu_lo_kernel(
         def gate_sum(t):
             for d in range(2):
                 pre[t, d] = sb("pre%d_%d" % (t, d), [P, T], F32)
-                nc.vector.tensor_tensor(pre[t, d][:], e_sb[t][:].indirect(lists[d][:]), y_sb[t][:], ALU.add)
+                for v0, v1 in ((0, T // 2), (T // 2, T)) if (t, d) == (0, 0) else ((0, T),):
+                    nc.vector.tensor_tensor(
+                        pre[t, d][:, v0:v1],
+                        e_sb[t][:].indirect(lists[d][:, v0 // 16 : v1 // 16]),
+                        y_sb[t][:, v0:v1],
+                        ALU.add,
+                    )
 
-        def gate_sigmoid(t):
-            for d in range(2):
-                gate[t, d] = sb("gate%d_%d" % (t, d), [P, T], F32)
-                nc.scalar.activation(gate[t, d][:], pre[t, d][:], ACT.Sigmoid)
+        def gate_sigmoid(t, d):
+            gate[t, d] = sb("gate%d_%d" % (t, d), [P, T], F32)
+            nc.scalar.activation(gate[t, d][:], pre[t, d][:], ACT.Sigmoid)
 
-        msg = {
-            (c, d): sb("msg%d_%d" % (c, d), [P, PACK * (v1 - v0)], F32)
-            for c, (v0, v1) in enumerate(CHUNKS)
-            for d in range(2)
-        }
+        msg = {}
+        msg_tag = ("msg0_%d", "pre3_%d")
 
         def messages(c, t):
             v0, v1 = CHUNKS[c]
             w = v1 - v0
             for d in range(2):
+                if t == 0:
+                    msg[c, d] = sb("msg%d_%d" % (c, d), [P, PACK * w], F32, tag=msg_tag[c] % d)
                 nc.vector.tensor_tensor(
                     msg[c, d][:, t * w : (t + 1) * w],
                     h_sb[t][:].indirect(lists[d][:, v0 // 16 : v1 // 16]),
@@ -130,93 +138,146 @@ def tile_picked_wgatedg_relu_lo_kernel(
 
         o_codes = sb("o_codes", [P, T], U32)
         o_scales = sb("o_scales", [P, T], U8)
-        total = {}
+        total = [sb("total%d" % c, [P, PACK * (v1 - v0)], F32) for c, (v0, v1) in enumerate(CHUNKS)]
         rounded = {}
         out_rows = out_0.rearrange("(p t) v -> p t v", t=PACK)
         out_words = out_1[0].rearrange("p c r -> p (c r)").bitcast(I32)
 
-        def add_up(c):
-            v0, v1 = CHUNKS[c]
-            total[c] = sb("total%d" % c, [P, PACK * (v1 - v0)], F32)
-            nc.vector.tensor_tensor(total[c][:], msg[c, 0][:], msg[c, 1][:], ALU.add)
+        res = {}
 
-        def round_out(c, engine):
+        turned = {}
+
+        def turn_sum(c, t, bank):
             v0, v1 = CHUNKS[c]
-            rounded[c] = sb("rounded%d" % c, [P, PACK * (v1 - v0)], BF16)
-            src = total[c][:].rearrange("p (t c i) -> p c t i", t=PACK, i=4)
-            dst = rounded[c][:].rearrange("p (c i t) -> p c t i", t=PACK, i=4)
+            w = v1 - v0
+            there = psum.tile([P, w], F32, name="there", tag="bank%d" % bank)
+            for b in range(0, w, P):
+                for d in range(2):
+                    nc.tensor.matmul(
+                        there[:, b : b + P],
+                        msg[c, d][:, t * w + b : t * w + b + P],
+                        ident[:],
+                        start=(d == 0),
+                        stop=(d == 1),
+                        is_transpose=True,
+                    )
+            turned[c, t] = sb("turned%d_%d" % (c, t), [P, w], F32)
+            nc.scalar.activation(turned[c, t][:], there[:], ACT.Relu)
+
+        def turn_back(c, t, bank):
+            v0, v1 = CHUNKS[c]
+            w = v1 - v0
+            back = psum.tile([P, w], F32, name="back", tag="bank%d" % bank)
+            for b in range(0, w, P):
+                nc.tensor.transpose(back[:, b : b + P], turned[c, t][:, b : b + P], ident[:])
+            nc.scalar.copy(out=total[c][:, t * w : (t + 1) * w], in_=back[:])
+
+        def add_on_vector(c, t0, t1):
+            v0, v1 = CHUNKS[c]
+            w = v1 - v0
+            cols = slice(t0 * w, t1 * w)
+            nc.vector.tensor_tensor(total[c][:, cols], msg[c, 0][:, cols], msg[c, 1][:, cols], ALU.add)
+
+        def relu(c, t0, t1):
+            w = CHUNKS[c][1] - CHUNKS[c][0]
+            nc.scalar.activation(res[c][:, t0 * w : t1 * w], total[c][:, t0 * w : t1 * w], ACT.Relu)
+
+        def round_out(c, a, b, engine):
+            v0, v1 = CHUNKS[c]
+            if a not in rounded:
+                rounded[a] = sb("rounded%d" % a, [P, PACK * (b - a)], BF16)[:]
+            dst = rounded[a].rearrange("p (c i t) -> p c t i", t=PACK, i=4)
+            src = total[c][:].rearrange("p (t c i) -> p c t i", t=PACK, i=4)[:, (a - v0) // 4 : (b - v0) // 4]
             if engine == "vector":
                 nc.vector.tensor_scalar_max(dst, src, 0.0)
             else:
                 nc.scalar.activation(dst, src, ACT.Relu)
 
-        def store_result(c):
+        def store_result(src, c, t0, t1):
             v0, v1 = CHUNKS[c]
-            res = sb("res%d" % c, [P, PACK * (v1 - v0)], F32)
-            nc.scalar.activation(res[:], total[c][:], ACT.Relu)
-            nc.sync.dma_start(out=out_rows[:, :, v0:v1], in_=res[:].rearrange("p (t v) -> p t v", t=PACK))
-
-        def store_codes(c):
-            v0, v1 = CHUNKS[c]
-            nc.vector.quantize_mx(
-                out=o_codes[:, v0:v1].bitcast(FP8X4), scales=o_scales[:, v0:v1], in_=rounded[c][:]
+            w = v1 - v0
+            nc.sync.dma_start(
+                out=out_rows[:, t0:t1, v0:v1], in_=src[:, t0 * w : t1 * w].rearrange("p (t v) -> p t v", v=w)
             )
-            nc.sync.dma_start(out=out_words[:, v0:v1], in_=o_codes[:, v0:v1].bitcast(I32))
+
+        def quantize_out(a, b):
+            nc.vector.quantize_mx(out=o_codes[:, a:b].bitcast(FP8X4), scales=o_scales[:, a:b], in_=rounded[a])
+
+        def store_codes(a, b):
+            nc.sync.dma_start(out=out_words[:, a:b], in_=o_codes[:, a:b].bitcast(I32))
 
         cast("vector", "e", 0, 2)
         cast("scalar", "e", 2, 4)
         quantize("e", 0)
-        project("e", 0, e_sb[0][:, :T])
+        project("e", 0, e_sb[0], 0)
         quantize("e", 2)
         cast("vector", "y", 0, 1)
-        cast("scalar", "y", 2, 4)
         quantize("y", 0)
-        project("y", 0, y_sb[0][:])
+        project("y", 0, y_sb[0], 3, 0, T // 2)
+        project("y", 0, y_sb[0], 4, T // 2, T)
         cast("vector", "y", 1, 2)
         quantize("y", 1)
+        project("e", 1, e_sb[1], 1)
+        project("y", 1, y_sb[1], 0)
+        cast("vector", "y", 2, 4)
         quantize("y", 2)
-        project("e", 1, e_sb[1][:, :T])
-        project("y", 1, y_sb[1][:])
-        gate_sum(0)
         cast("scalar", "h", 0, 2)
+        project("e", 2, e_sb[2], 2)
+        gate_sum(0)
         quantize("h", 0)
-        gate_sigmoid(0)
+        gate_sigmoid(0, 0)
         gate_sum(1)
-        project("h", 0, h_sb[0][:])
-        project("e", 2, e_sb[2][:, :T])
-        project("y", 2, y_sb[2][:])
-        gate_sigmoid(1)
-        project("h", 1, h_sb[1][:])
-        messages(0, 0)
-        gate_sum(2)
+        gate_sigmoid(0, 1)
+        project("h", 0, h_sb[0], 5)
         cast("scalar", "h", 2, 4)
+        messages(0, 0)
         quantize("h", 2)
-        project("e", 3, e_sb[3][:, :T])
-        project("y", 3, y_sb[3][:])
+        project("y", 2, y_sb[2], 5)
+        gate_sigmoid(1, 0)
+        gate_sigmoid(1, 1)
+        project("h", 1, h_sb[1], 0)
+        gate_sum(2)
         messages(0, 1)
-        gate_sigmoid(2)
+        project("e", 3, e_sb[3], 3)
+        project("y", 3, y_sb[3], 0)
         gate_sum(3)
-        project("h", 2, h_sb[2][:])
-        project("h", 3, h_sb[3][:])
-        gate_sigmoid(3)
+        turn_sum(0, 0, 6)
+        project("h", 2, h_sb[2], 1)
+        project("h", 3, h_sb[3], 2)
+        turn_back(0, 0, 5)
+        gate_sigmoid(2, 0)
+        gate_sigmoid(2, 1)
         messages(0, 2)
+        turn_sum(0, 1, 7)
+        gate_sigmoid(3, 0)
+        turn_back(0, 1, 4)
+        gate_sigmoid(3, 1)
         messages(0, 3)
-        add_up(0)
-        round_out(0, "scalar")
-        store_result(0)
-        for t in range(PACK):
+        add_on_vector(0, 3, 4)
+        turn_sum(0, 2, 3)
+        turn_back(0, 2, 0)
+        store_result(total[0], 0, 0, 3)
+        round_out(0, 0, 256, "scalar")
+        round_out(0, 256, 384, "scalar")
+        top = sb("top", [P, 384], F32, tag="turned0_2")
+        nc.scalar.activation(top[:], total[0][:, 3 * 384 :], ACT.Relu)
+        nc.sync.dma_start(out=out_rows[:, 3, 0:384], in_=top[:])
+        for t in range(PACK - 1):
             messages(1, t)
-        add_up(1)
-        store_codes(0)
-        round_out(1, "scalar")
-        store_result(1)
-        for t in range(PACK):
-            messages(2, t)
-        add_up(2)
-        store_codes(1)
-        round_out(2, "vector")
-        store_result(2)
-        store_codes(2)
+        add_on_vector(1, 0, PACK - 1)
+        messages(1, PACK - 1)
+        add_on_vector(1, PACK - 1, PACK)
+        quantize_out(0, 256)
+        last = sb("last", [P, 768], F32, tag="rounded0")
+        res[1] = last[:, :512]
+        rounded[384] = last[:, 512:].bitcast(BF16)
+        quantize_out(256, 384)
+        store_codes(0, 384)
+        round_out(1, 384, 512, "vector")
+        relu(1, 0, 4)
+        store_result(res[1], 1, 0, 4)
+        quantize_out(384, 512)
+        store_codes(384, 512)
         for q in range(4):
             queue = nc.scalar if q % 2 else nc.sync
             queue.dma_start(

@@ -69,8 +69,8 @@ def tile_picked_wgatedg_relu_lo_kernel(
         grouped = {}
         stationary = {}
 
-        def cast(engine, n, t0, t1):
-            g = sb("g_%s%d" % (n, t0), [P, (t1 - t0) * N], BF16)
+        def cast(engine, n, t0, t1, tag=""):
+            g = sb("g_%s%d" % (n, t0), [P, (t1 - t0) * N], BF16, tag=tag)
             grouped[n, t0] = (g, t1)
             src = raw[n][:].rearrange("p j (m t) -> p m t j", t=PACK)[:, :, t0:t1, :]
             dst = g[:].rearrange("p (t m j) -> p m t j", m=P, j=PACK)
@@ -211,47 +211,43 @@ def tile_picked_wgatedg_relu_lo_kernel(
         quantize("e", 0)
         project("e", 0, e_sb[0], 0)
         quantize("e", 2)
-        cast("vector", "y", 0, 1)
+        project("e", 1, e_sb[1], 1)
+        project("e", 2, e_sb[2], 2)
+        cast("vector", "y", 0, 2)
         quantize("y", 0)
         project("y", 0, y_sb[0], 3, 0, T // 2)
         project("y", 0, y_sb[0], 4, T // 2, T)
-        cast("vector", "y", 1, 2)
-        quantize("y", 1)
-        project("e", 1, e_sb[1], 1)
         project("y", 1, y_sb[1], 0)
-        cast("vector", "y", 2, 4)
+        cast("vector", "y", 2, 4, "g_y0")
         quantize("y", 2)
-        cast("scalar", "h", 0, 2)
-        project("e", 2, e_sb[2], 2)
         gate_sum(0)
-        quantize("h", 0)
-        gate_sigmoid(0, 0)
+        project("y", 2, y_sb[2], 1)
         gate_sum(1)
-        gate_sigmoid(0, 1)
-        project("h", 0, h_sb[0], 5)
-        cast("scalar", "h", 2, 4)
-        messages(0, 0)
-        quantize("h", 2)
-        project("y", 2, y_sb[2], 5)
-        gate_sigmoid(1, 0)
-        gate_sigmoid(1, 1)
-        project("h", 1, h_sb[1], 0)
+        cast("scalar", "h", 0, 4, "y0")
         gate_sum(2)
-        messages(0, 1)
-        project("e", 3, e_sb[3], 3)
+        quantize("h", 0)
+        project("e", 3, e_sb[3], 1)
         project("y", 3, y_sb[3], 0)
         gate_sum(3)
-        turn_sum(0, 0, 6)
-        project("h", 2, h_sb[2], 1)
-        project("h", 3, h_sb[3], 2)
-        turn_back(0, 0, 5)
+        gate_sigmoid(0, 0)
+        gate_sigmoid(0, 1)
+        project("h", 0, h_sb[0], 4)
+        messages(0, 0)
+        gate_sigmoid(1, 0)
+        gate_sigmoid(1, 1)
+        project("h", 1, h_sb[1], 5)
+        messages(0, 1)
         gate_sigmoid(2, 0)
         gate_sigmoid(2, 1)
+        project("h", 2, h_sb[2], 2)
         messages(0, 2)
-        turn_sum(0, 1, 7)
+        project("h", 3, h_sb[3], 3)
+        turn_sum(0, 0, 6)
         gate_sigmoid(3, 0)
-        turn_back(0, 1, 4)
         gate_sigmoid(3, 1)
+        turn_back(0, 0, 5)
+        turn_sum(0, 1, 7)
+        turn_back(0, 1, 4)
         messages(0, 3)
         add_on_vector(0, 3, 4)
         turn_sum(0, 2, 3)
@@ -268,14 +264,12 @@ def tile_picked_wgatedg_relu_lo_kernel(
         messages(1, PACK - 1)
         add_on_vector(1, PACK - 1, PACK)
         quantize_out(0, 256)
-        last = sb("last", [P, 768], F32, tag="rounded0")
-        res[1] = last[:, :512]
-        rounded[384] = last[:, 512:].bitcast(BF16)
+        res[1] = sb("res1", [P, 512], F32)
+        nc.vector.tensor_scalar_max(res[1][:], total[1][:], 0.0)
+        store_result(res[1], 1, 0, 4)
+        round_out(1, 384, 512, "scalar")
         quantize_out(256, 384)
         store_codes(0, 384)
-        round_out(1, 384, 512, "vector")
-        relu(1, 0, 4)
-        store_result(res[1], 1, 0, 4)
         quantize_out(384, 512)
         store_codes(384, 512)
         for q in range(4):

@@ -38,7 +38,7 @@ def tile_picked_wgatedg_relu_lo_kernel(
         xw = sb("xw", [P, 2 * T], U8)
         xs = sb("xs", [P, T], U8)
         zero = sb("zero", [P, SPARE], F32)
-        raw = {n: sb("raw_" + n, [P, PACK, N], F32) for n in "eyh"}
+        raw = {}
         e_sb = [sb("e%d" % t, [P, T + SPARE], F32) for t in range(PACK)]
         y_sb = [sb("y%d" % t, [P, T], F32) for t in range(PACK)]
         h_sb = [sb("h%d" % t, [P, T], F32) for t in range(PACK)]
@@ -51,39 +51,41 @@ def tile_picked_wgatedg_relu_lo_kernel(
         ident = sb("ident", [P, P], F32)
         make_identity(nc, ident[:])
 
-        def load_w(n, w):
-            nc.sync.dma_start(out=raw[n][:], in_=w.rearrange("(p j) c -> p j c", j=PACK))
+        def load_w(n, w, m0=0, m1=P):
+            raw[n, m0] = sb("raw_%s%d" % (n, m0), [P, PACK, PACK * (m1 - m0)], F32)
+            rows = w.rearrange("(p j) c -> p j c", j=PACK)
+            nc.sync.dma_start(out=raw[n, m0][:], in_=rows[:, :, PACK * m0 : PACK * m1])
 
-        nc.sync.dma_start(out=xw[:].bitcast(I32), in_=x_words[0].bitcast(I32))
-        nc.sync.dma_start(lists[0][:], pos1)
         load_w("e", w2)
+        load_w("y", w1)
+        nc.sync.dma_start(out=xw[:].bitcast(I32), in_=x_words[0].bitcast(I32))
         for q in range(4):
             nc.sync.dma_start(
                 out=xs[32 * q : 32 * q + 4, :].bitcast(I32),
                 in_=x_scales[0, 4 * q : 4 * q + 4, :].bitcast(I32),
             )
-        load_w("y", w1)
+        nc.sync.dma_start(lists[0][:], pos1)
         nc.sync.dma_start(lists[1][:], pos2)
         load_w("h", w3)
 
         grouped = {}
         stationary = {}
 
-        def cast(engine, n, t0, t1, tag=""):
-            g = sb("g_%s%d" % (n, t0), [P, (t1 - t0) * N], BF16, tag=tag)
-            grouped[n, t0] = (g, t1)
-            src = raw[n][:].rearrange("p j (m t) -> p m t j", t=PACK)[:, :, t0:t1, :]
-            dst = g[:].rearrange("p (t m j) -> p m t j", m=P, j=PACK)
+        def cast(engine, n, t0, t1, tag="", m0=0, m1=P):
+            if (n, t0) not in grouped:
+                grouped[n, t0] = sb("g_%s%d" % (n, t0), [P, (t1 - t0) * N], BF16, tag=tag)
+            src = raw[n, m0][:].rearrange("p j (m t) -> p m t j", t=PACK)[:, :, t0:t1, :]
+            dst = grouped[n, t0][:].rearrange("p (t m j) -> p m t j", m=P, j=PACK)[:, m0:m1]
             if engine == "vector":
                 nc.vector.tensor_copy(out=dst, in_=src)
             else:
                 nc.scalar.copy(out=dst, in_=src)
 
-        def quantize(n, t0):
-            g, t1 = grouped[n, t0]
+        def quantize(n, g0, t0, t1):
             codes = sb("c_%s%d" % (n, t0), [P, (t1 - t0) * P], U32)
             scales = sb("s_%s%d" % (n, t0), [P, (t1 - t0) * P], U8)
-            nc.vector.quantize_mx(out=codes[:].bitcast(FP8X4), scales=scales[:], in_=g[:])
+            src = grouped[n, g0][:, (t0 - g0) * N : (t1 - g0) * N]
+            nc.vector.quantize_mx(out=codes[:].bitcast(FP8X4), scales=scales[:], in_=src)
             for t in range(t0, t1):
                 cols = slice((t - t0) * P, (t - t0 + 1) * P)
                 stationary[n, t] = (codes[:, cols], scales[:, cols])
@@ -117,7 +119,7 @@ def tile_picked_wgatedg_relu_lo_kernel(
                     )
 
         def gate_sigmoid(t, d):
-            gate[t, d] = sb("gate%d_%d" % (t, d), [P, T], F32)
+            gate[t, d] = sb("gate%d_%d" % (t, d), [P, T], F32, tag="c_e0" if (t, d) == (0, 0) else "")
             nc.scalar.activation(gate[t, d][:], pre[t, d][:], ACT.Sigmoid)
 
         msg = {}
@@ -208,34 +210,35 @@ def tile_picked_wgatedg_relu_lo_kernel(
 
         cast("vector", "e", 0, 2)
         cast("scalar", "e", 2, 4)
-        quantize("e", 0)
+        quantize("e", 0, 0, 2)
+        quantize("e", 2, 2, 4)
+        cast("scalar", "y", 2, 4)
         project("e", 0, e_sb[0], 0)
-        quantize("e", 2)
-        project("e", 1, e_sb[1], 1)
-        project("e", 2, e_sb[2], 2)
         cast("vector", "y", 0, 2)
-        quantize("y", 0)
+        quantize("y", 0, 0, 1)
         project("y", 0, y_sb[0], 3, 0, T // 2)
         project("y", 0, y_sb[0], 4, T // 2, T)
-        project("y", 1, y_sb[1], 0)
-        cast("vector", "y", 2, 4, "g_y0")
-        quantize("y", 2)
+        quantize("y", 0, 1, 2)
+        project("y", 1, y_sb[1], 2)
+        project("e", 1, e_sb[1], 0)
+        quantize("y", 2, 2, 4)
         gate_sum(0)
-        project("y", 2, y_sb[2], 1)
+        project("e", 2, e_sb[2], 3)
+        project("y", 2, y_sb[2], 4)
         gate_sum(1)
         cast("scalar", "h", 0, 4, "y0")
         gate_sum(2)
-        quantize("h", 0)
-        project("e", 3, e_sb[3], 1)
-        project("y", 3, y_sb[3], 0)
+        quantize("h", 0, 0, 4)
+        project("e", 3, e_sb[3], 3)
+        project("y", 3, y_sb[3], 4)
         gate_sum(3)
         gate_sigmoid(0, 0)
         gate_sigmoid(0, 1)
-        project("h", 0, h_sb[0], 4)
+        project("h", 0, h_sb[0], 0)
         messages(0, 0)
         gate_sigmoid(1, 0)
         gate_sigmoid(1, 1)
-        project("h", 1, h_sb[1], 5)
+        project("h", 1, h_sb[1], 1)
         messages(0, 1)
         gate_sigmoid(2, 0)
         gate_sigmoid(2, 1)
@@ -267,11 +270,11 @@ def tile_picked_wgatedg_relu_lo_kernel(
         res[1] = sb("res1", [P, 512], F32)
         nc.vector.tensor_scalar_max(res[1][:], total[1][:], 0.0)
         store_result(res[1], 1, 0, 4)
+        store_codes(0, 256)
         round_out(1, 384, 512, "scalar")
         quantize_out(256, 384)
-        store_codes(0, 384)
         quantize_out(384, 512)
-        store_codes(384, 512)
+        store_codes(256, 512)
         for q in range(4):
             queue = nc.scalar if q % 2 else nc.sync
             queue.dma_start(

from contextlib import ExitStack

import concourse.mybir as mybir
from concourse.masks import make_identity

K, T, N = 512, 512, 512
FLOPS = 3 * 2 * K * T * N

F32 = mybir.dt.float32
BF16 = mybir.dt.bfloat16
I32 = mybir.dt.int32
U32 = mybir.dt.uint32
U16 = mybir.dt.uint16
U8 = mybir.dt.uint8
FP8X4 = mybir.dt.float8_e4m3fn_x4
FP4X4 = mybir.dt.float4_e2m1fn_x4
ACT = mybir.ActivationFunctionType
ALU = mybir.AluOpType

P = 128
PACK = 4
SPARE = 8
CHUNKS = ((0, 384), (384, 512))


def tile_picked_wgatedg_relu_lo_kernel(
    tc, x_words, x_scales, w1, w2, w3, pos1, pos2, out_0, out_1, out_2
):
    nc = tc.nc
    with ExitStack() as ctx:
        keep = ctx.enter_context(tc.tile_pool(name="keep", bufs=1))
        psum = ctx.enter_context(tc.psum_pool(name="psum", bufs=1))

        def sb(name, shape, dtype, tag=""):
            return keep.tile(shape, dtype, name=name, tag=tag or name, align_bytes=64)

        lists = [sb("list%d" % d, [P, T // 16], U16) for d in range(2)]
        xw = sb("xw", [P, 2 * T], U8)
        xs = sb("xs", [P, T], U8)
        zero = sb("zero", [P, SPARE], F32)
        raw = {}
        e_sb = [sb("e%d" % t, [P, T + SPARE], F32) for t in range(PACK)]
        y_sb = [sb("y%d" % t, [P, T], F32) for t in range(PACK)]
        h_sb = [sb("h%d" % t, [P, T], F32) for t in range(PACK)]

        nc.vector.memset(xs[:].bitcast(I32), 0)
        nc.vector.memset(zero[:], 0.0)
        for t in range(PACK):
            nc.scalar.activation(e_sb[t][:, T:], zero[:], ACT.Sigmoid)

        ident = sb("ident", [P, P], F32)
        make_identity(nc, ident[:])

        def load_w(n, w, m0=0, m1=P):
            raw[n, m0] = sb("raw_%s%d" % (n, m0), [P, PACK, PACK * (m1 - m0)], F32)
            rows = w.rearrange("(p j) c -> p j c", j=PACK)
            nc.sync.dma_start(out=raw[n, m0][:], in_=rows[:, :, PACK * m0 : PACK * m1])

        load_w("e", w2)
        load_w("y", w1)
        nc.sync.dma_start(out=xw[:].bitcast(I32), in_=x_words[0].bitcast(I32))
        for q in range(4):
            nc.sync.dma_start(
                out=xs[32 * q : 32 * q + 4, :].bitcast(I32),
                in_=x_scales[0, 4 * q : 4 * q + 4, :].bitcast(I32),
            )
        nc.sync.dma_start(lists[0][:], pos1)
        nc.sync.dma_start(lists[1][:], pos2)
        load_w("h", w3)

        grouped = {}
        stationary = {}

        def cast(engine, n, t0, t1, tag="", m0=0, m1=P):
            if (n, t0) not in grouped:
                grouped[n, t0] = sb("g_%s%d" % (n, t0), [P, (t1 - t0) * N], BF16, tag=tag)
            src = raw[n, m0][:].rearrange("p j (m t) -> p m t j", t=PACK)[:, :, t0:t1, :]
            dst = grouped[n, t0][:].rearrange("p (t m j) -> p m t j", m=P, j=PACK)[:, m0:m1]
            if engine == "vector":
                nc.vector.tensor_copy(out=dst, in_=src)
            else:
                nc.scalar.copy(out=dst, in_=src)

        def quantize(n, g0, t0, t1):
            codes = sb("c_%s%d" % (n, t0), [P, (t1 - t0) * P], U32)
            scales = sb("s_%s%d" % (n, t0), [P, (t1 - t0) * P], U8)
            src = grouped[n, g0][:, (t0 - g0) * N : (t1 - g0) * N]
            nc.vector.quantize_mx(out=codes[:].bitcast(FP8X4), scales=scales[:], in_=src)
            for t in range(t0, t1):
                cols = slice((t - t0) * P, (t - t0 + 1) * P)
                stationary[n, t] = (codes[:, cols], scales[:, cols])

        def project(n, t, dst, bank, v0=0, v1=T):
            codes, scales = stationary[n, t]
            acc = psum.tile([P, v1 - v0], F32, name="acc", tag="bank%d" % bank)
            nc.tensor.matmul_mx(
                out=acc[:],
                lhsT=codes.bitcast(FP8X4),
                lhsT_scale=scales,
                rhs=xw[:, 2 * v0 : 2 * v1].bitcast(FP4X4),
                rhs_scale=xs[:, v0:v1],
                start=True,
                stop=True,
            )
            nc.scalar.copy(out=dst[:, v0:v1], in_=acc[:])

        pre = {}
        gate = {}

        def gate_sum(t):
            for d in range(2):
                pre[t, d] = sb("pre%d_%d" % (t, d), [P, T], F32)
                for v0, v1 in ((0, T // 2), (T // 2, T)) if (t, d) == (0, 0) else ((0, T),):
                    nc.vector.tensor_tensor(
                        pre[t, d][:, v0:v1],
                        e_sb[t][:].indirect(lists[d][:, v0 // 16 : v1 // 16]),
                        y_sb[t][:, v0:v1],
                        ALU.add,
                    )

        def gate_sigmoid(t, d):
            gate[t, d] = sb("gate%d_%d" % (t, d), [P, T], F32, tag="c_e0" if (t, d) == (0, 0) else "")
            nc.scalar.activation(gate[t, d][:], pre[t, d][:], ACT.Sigmoid)

        msg = {}
        msg_tag = ("msg0_%d", "pre3_%d")

        def messages(c, t):
            v0, v1 = CHUNKS[c]
            w = v1 - v0
            for d in range(2):
                if t == 0:
                    msg[c, d] = sb("msg%d_%d" % (c, d), [P, PACK * w], F32, tag=msg_tag[c] % d)
                nc.vector.tensor_tensor(
                    msg[c, d][:, t * w : (t + 1) * w],
                    h_sb[t][:].indirect(lists[d][:, v0 // 16 : v1 // 16]),
                    gate[t, d][:, v0:v1],
                    ALU.mult,
                )

        o_codes = sb("o_codes", [P, T], U32)
        o_scales = sb("o_scales", [P, T], U8)
        total = [sb("total%d" % c, [P, PACK * (v1 - v0)], F32) for c, (v0, v1) in enumerate(CHUNKS)]
        rounded = {}
        out_rows = out_0.rearrange("(p t) v -> p t v", t=PACK)
        out_words = out_1[0].rearrange("p c r -> p (c r)").bitcast(I32)

        res = {}

        turned = {}

        def turn_sum(c, t, bank):
            v0, v1 = CHUNKS[c]
            w = v1 - v0
            there = psum.tile([P, w], F32, name="there", tag="bank%d" % bank)
            for b in range(0, w, P):
                for d in range(2):
                    nc.tensor.matmul(
                        there[:, b : b + P],
                        msg[c, d][:, t * w + b : t * w + b + P],
                        ident[:],
                        start=(d == 0),
                        stop=(d == 1),
                        is_transpose=True,
                    )
            turned[c, t] = sb("turned%d_%d" % (c, t), [P, w], F32)
            nc.scalar.activation(turned[c, t][:], there[:], ACT.Relu)

        def turn_back(c, t, bank):
            v0, v1 = CHUNKS[c]
            w = v1 - v0
            back = psum.tile([P, w], F32, name="back", tag="bank%d" % bank)
            for b in range(0, w, P):
                nc.tensor.transpose(back[:, b : b + P], turned[c, t][:, b : b + P], ident[:])
            nc.scalar.copy(out=total[c][:, t * w : (t + 1) * w], in_=back[:])

        def add_on_vector(c, t0, t1):
            v0, v1 = CHUNKS[c]
            w = v1 - v0
            cols = slice(t0 * w, t1 * w)
            nc.vector.tensor_tensor(total[c][:, cols], msg[c, 0][:, cols], msg[c, 1][:, cols], ALU.add)

        def relu(c, t0, t1):
            w = CHUNKS[c][1] - CHUNKS[c][0]
            nc.scalar.activation(res[c][:, t0 * w : t1 * w], total[c][:, t0 * w : t1 * w], ACT.Relu)

        def round_out(c, a, b, engine):
            v0, v1 = CHUNKS[c]
            if a not in rounded:
                rounded[a] = sb("rounded%d" % a, [P, PACK * (b - a)], BF16)[:]
            dst = rounded[a].rearrange("p (c i t) -> p c t i", t=PACK, i=4)
            src = total[c][:].rearrange("p (t c i) -> p c t i", t=PACK, i=4)[:, (a - v0) // 4 : (b - v0) // 4]
            if engine == "vector":
                nc.vector.tensor_scalar_max(dst, src, 0.0)
            else:
                nc.scalar.activation(dst, src, ACT.Relu)

        def store_result(src, c, t0, t1):
            v0, v1 = CHUNKS[c]
            w = v1 - v0
            nc.sync.dma_start(
                out=out_rows[:, t0:t1, v0:v1], in_=src[:, t0 * w : t1 * w].rearrange("p (t v) -> p t v", v=w)
            )

        def quantize_out(a, b):
            nc.vector.quantize_mx(out=o_codes[:, a:b].bitcast(FP8X4), scales=o_scales[:, a:b], in_=rounded[a])

        def store_codes(a, b):
            nc.sync.dma_start(out=out_words[:, a:b], in_=o_codes[:, a:b].bitcast(I32))

        cast("vector", "e", 0, 2)
        cast("scalar", "e", 2, 4)
        quantize("e", 0, 0, 2)
        quantize("e", 2, 2, 4)
        cast("scalar", "y", 2, 4)
        project("e", 0, e_sb[0], 0)
        cast("vector", "y", 0, 2)
        quantize("y", 0, 0, 1)
        project("y", 0, y_sb[0], 3, 0, T // 2)
        project("y", 0, y_sb[0], 4, T // 2, T)
        quantize("y", 0, 1, 2)
        project("y", 1, y_sb[1], 2)
        project("e", 1, e_sb[1], 0)
        quantize("y", 2, 2, 4)
        gate_sum(0)
        project("e", 2, e_sb[2], 3)
        project("y", 2, y_sb[2], 4)
        gate_sum(1)
        cast("scalar", "h", 0, 4, "y0")
        gate_sum(2)
        quantize("h", 0, 0, 4)
        project("e", 3, e_sb[3], 3)
        project("y", 3, y_sb[3], 4)
        gate_sum(3)
        gate_sigmoid(0, 0)
        gate_sigmoid(0, 1)
        project("h", 0, h_sb[0], 0)
        messages(0, 0)
        gate_sigmoid(1, 0)
        gate_sigmoid(1, 1)
        project("h", 1, h_sb[1], 1)
        messages(0, 1)
        gate_sigmoid(2, 0)
        gate_sigmoid(2, 1)
        project("h", 2, h_sb[2], 2)
        messages(0, 2)
        project("h", 3, h_sb[3], 3)
        turn_sum(0, 0, 6)
        gate_sigmoid(3, 0)
        gate_sigmoid(3, 1)
        turn_back(0, 0, 5)
        turn_sum(0, 1, 7)
        turn_back(0, 1, 4)
        messages(0, 3)
        add_on_vector(0, 3, 4)
        turn_sum(0, 2, 3)
        turn_back(0, 2, 0)
        store_result(total[0], 0, 0, 3)
        round_out(0, 0, 256, "scalar")
        round_out(0, 256, 384, "scalar")
        top = sb("top", [P, 384], F32, tag="turned0_2")
        nc.scalar.activation(top[:], total[0][:, 3 * 384 :], ACT.Relu)
        nc.sync.dma_start(out=out_rows[:, 3, 0:384], in_=top[:])
        for t in range(PACK - 1):
            messages(1, t)
        add_on_vector(1, 0, PACK - 1)
        messages(1, PACK - 1)
        add_on_vector(1, PACK - 1, PACK)
        quantize_out(0, 256)
        res[1] = sb("res1", [P, 512], F32)
        nc.vector.tensor_scalar_max(res[1][:], total[1][:], 0.0)
        store_result(res[1], 1, 0, 4)
        store_codes(0, 256)
        round_out(1, 384, 512, "scalar")
        quantize_out(256, 384)
        quantize_out(384, 512)
        store_codes(256, 512)
        for q in range(4):
            queue = nc.scalar if q % 2 else nc.sync
            queue.dma_start(
                out=out_2[0, 4 * q : 4 * q + 4, :].bitcast(I32),
                in_=o_scales[32 * q : 32 * q + 4, :].bitcast(I32),
            )
